import numpy as np
import ml_dtypes


def mxq(x, axis, fmt="e4m3"):
    dtype, down = {"e4m3": (ml_dtypes.float8_e4m3fn, 7), "e5m2": (ml_dtypes.float8_e5m2, 14)}[fmt]
    v = np.moveaxis(np.asarray(x, np.float32).astype(ml_dtypes.bfloat16).astype(np.float64), axis, -1)
    blocks = v.reshape(v.shape[:-1] + (-1, 32))
    amax = np.abs(blocks).max(-1, keepdims=True)
    byte = np.maximum(np.where(amax > 0, np.frexp(amax)[1] - 1 + 127, 0) - down, 1)
    scale = np.exp2(byte - 127.0)
    codes = (blocks / scale).astype(np.float32).astype(dtype).astype(np.float64)
    return np.moveaxis((codes * scale).reshape(v.shape), -1, axis)


WIDE = False


def mx_kscale(k):
    if not WIDE:
        return np.ones(k)
    levels = np.array([10, -10, 5, -5, 0])
    if k % 512:
        return np.exp2(np.random.permutation(np.resize(levels, k // 32))).repeat(32)
    a = np.empty((k // 512, 16))
    for p in range(k // 512):
        a[p, :8] = np.random.permutation(np.resize(levels, 8))
        for g in range(8):
            far = levels[np.abs(levels - a[p, g]) >= 10]
            a[p, g + 8] = far[np.random.randint(len(far))]
    return np.exp2(a.ravel()).repeat(32)


BF16 = ml_dtypes.bfloat16


def bf(x):
    return np.asarray(x, np.float32).astype(BF16)


def f64(x):
    return np.asarray(x).astype(np.float64)


E2M1 = np.array([0.0, 0.5, 1.0, 1.5, 2.0, 3.0, 4.0, 6.0, -0.0, -0.5, -1.0, -1.5, -2.0, -3.0, -4.0, -6.0])


def pack_weight(w, fmt):
    k, n = w.shape
    w = f64(bf(w)).reshape(k // 32, 32, n)
    amax = np.abs(w).max(1)
    if fmt == "e4m3":
        byte = np.frexp(amax)[1] - 1 + 127 - 7
    else:
        mant, ex = np.frexp(amax / 6.0)
        byte = np.where(mant > 0.5, ex, ex - 1) + 127
    byte = np.clip(np.where(amax > 0, byte, 1), 1, 254)
    scaled = (w * np.exp2(127.0 - byte)[:, None, :]).reshape(k, n).astype(np.float32)
    by_word = np.ascontiguousarray(scaled.reshape(k // 512, 128, 4, n).transpose(0, 1, 3, 2))
    if fmt == "e4m3":
        words = by_word.astype(ml_dtypes.float8_e4m3fn).view(np.uint8)
    else:
        c = by_word.astype(ml_dtypes.float4_e2m1fn).view(np.uint8) & 0xF
        words = c[..., 0::2] | (c[..., 1::2] << 4)
    return np.ascontiguousarray(words), np.ascontiguousarray(byte.astype(np.uint8).reshape(k // 512, 16, n))


def unpack_weight(words, scales, fmt):
    g, p, n, _ = words.shape
    if fmt == "e4m3":
        vals = np.ascontiguousarray(words).view(ml_dtypes.float8_e4m3fn).astype(np.float64)
    else:
        nib = np.empty((g, p, n, 4), np.uint8)
        nib[..., 0::2] = words & 0xF
        nib[..., 1::2] = words >> 4
        vals = E2M1[nib]
    vals = vals * np.repeat(np.exp2(scales.astype(np.float64) - 127.0), 8, axis=1)[..., None]
    return vals.transpose(0, 1, 3, 2).reshape(g * 512, n)
def pack4(w):
    words, scales = pack_weight(w, "e2m1")
    return words.reshape(words.shape[0], 128, -1), scales


def unpack4(words, scales):
    return unpack_weight(words.reshape(words.shape[0], 128, -1, 2), scales, "e2m1")


N, D, E, T = 1024, 1024, 512, 1024


def draw0():
    s = mx_kscale(D)
    u = mx_kscale(N)
    h = bf(np.random.standard_normal((N, D)) * s)
    e = bf(np.random.standard_normal((N, E)) / u[:, None])
    y = bf(np.random.standard_normal((N, T)))
    nu = bf(np.random.uniform(3.0, 8.0, T))
    wm_words, wm_scales = pack4(np.random.standard_normal((D, T)) / np.sqrt(D) / s[:, None])
    ws_words, ws_scales = pack4(0.4 * np.random.standard_normal((D, T)) / np.sqrt(D) / s[:, None])
    g = bf((1.0 + 0.1 * np.random.standard_normal(N)) * u)
    return {
        "h": h,
        "e": e,
        "y": y,
        "nu": nu,
        "wm_words": wm_words,
        "wm_scales": wm_scales,
        "ws_words": ws_words,
        "ws_scales": ws_scales,
        "g": g,
    }


def student_nll_grads(a, c, y, nu):
    p = np.exp(c)
    z = (y - a) * p
    z2 = z * z
    w = (nu + 1.0)[None, :] / (nu[None, :] + z2)
    da = -w * z * p
    dc = w * z2 - 1.0
    return da, dc


def core(h, e, y, nu, wm_words, wm_scales, ws_words, ws_scales, g):
    n = e.shape[0]
    root_n = np.sqrt(n)
    g = f64(g)

    hq = mxq(f64(h), 1, "e4m3")
    a = hq @ unpack4(wm_words, wm_scales)
    c = hq @ unpack4(ws_words, ws_scales)

    da, dc = student_nll_grads(a, c, f64(y), f64(nu))

    ga = g[:, None] * da
    gc = g[:, None] * dc

    eq = mxq(f64(e), 0, "e4m3")
    gvm = (eq.T @ mxq(ga, 0, "e4m3")) / root_n
    gvs = (eq.T @ mxq(gc, 0, "e4m3")) / root_n
    return gvm, gvs


def e4m3fn_bytes(y):
    return np.clip(np.asarray(y, np.float64), -448.0, 448.0).astype(np.float32).astype(ml_dtypes.float8_e4m3fn).view(np.uint8)


def e4m3fn_values(b):
    return np.asarray(b, np.uint8).view(ml_dtypes.float8_e4m3fn).astype(np.float64)


def setup_inputs():
    d = draw0()
    x0 = np.asarray(d['h']).astype(np.float64)
    s = (np.max(np.abs(x0), axis=(0,), keepdims=True) / 448.0).astype(np.float32)
    out = {}
    for k, v in d.items():
        if k == 'h':
            out['h_bytes'] = e4m3fn_bytes(x0 / s.astype(np.float64))
            out['h_scale'] = s
        else:
            out[k] = v
    return out


def reference(h_bytes, h_scale, e, y, nu, wm_words, wm_scales, ws_words, ws_scales, g):
    return core(e4m3fn_values(h_bytes) * h_scale.astype(np.float64), e, y, nu, wm_words, wm_scales, ws_words, ws_scales, g)

@@ -1,0 +1,450 @@
+from contextlib import ExitStack
+
+import concourse.mybir as mybir
+from concourse.masks import make_identity
+
+N, D, E, T = 1024, 1024, 512, 1024
+FLOPS = 2 * 2 * N * D * T + 2 * 2 * E * N * T
+
+F32 = mybir.dt.float32
+BF16 = mybir.dt.bfloat16
+I32 = mybir.dt.int32
+U32 = mybir.dt.uint32
+U8 = mybir.dt.uint8
+FP8 = mybir.dt.float8_e4m3fn
+FP8X4 = mybir.dt.float8_e4m3fn_x4
+FP4X4 = mybir.dt.float4_e2m1fn_x4
+ACT = mybir.ActivationFunctionType
+ALU = mybir.AluOpType
+
+P = 128
+PACK = 4
+PASS = P * PACK
+GROUPS = N // PASS
+K_PASSES = D // PASS
+T_TILES = T // P
+E_TILES = E // P
+W = 256
+SUBS = W // P
+CHUNKS = (T // W) * GROUPS
+OUT_SCALE = 1.0 / 32.0
+
+
+def tile_deeparstudentheadgradient_w4_kernel(
+    tc, h_bytes, h_scale, e, y, nu, wm_words, wm_scales, ws_words, ws_scales, g, out_0, out_1
+):
+    nc = tc.nc
+    with ExitStack() as ctx:
+        keep = ctx.enter_context(tc.tile_pool(name="keep", bufs=1))
+        work = ctx.enter_context(tc.tile_pool(name="work", bufs=3))
+        psum = ctx.enter_context(tc.psum_pool(name="psum", bufs=8))
+        ctx.enter_context(tc.manual_schedule())
+
+        def bank(name):
+            return psum.tile([P, PASS], F32, name=name, tag="bank")
+
+        ident = keep.tile([P, P], F32, name="ident")
+        make_identity(nc, ident[:])
+        nu_rows = keep.tile([P, P], F32, name="nu_rows")
+        nc.gpsimd.memset(nu_rows[:], 0.0)
+
+        ws_sc = keep.tile([P, K_PASSES, T], U8, name="ws_sc", align_bytes=64)
+        wm_sc = keep.tile([P, K_PASSES, T], U8, name="wm_sc", align_bytes=64)
+        nc.vector.memset(ws_sc[:].bitcast(I32), 0)
+        nc.vector.memset(wm_sc[:].bitcast(I32), 0)
+
+        hs_raw = keep.tile([P, 8], F32, name="hs_raw")
+        nc.sync.dma_start(out=hs_raw[:], in_=h_scale.rearrange("o (p c) -> p (o c)", c=8))
+        h_rows = h_bytes.rearrange("(g p jj j) k -> g jj p (j k)", g=GROUPS, p=P, jj=2)
+        h_raw = []
+
+        def load_h(i):
+            h_tile = keep.tile([P, 2 * D], U8, name="h_raw%d" % i)
+            nc.sync.dma_start(out=h_tile[:], in_=h_rows[i // 2, i % 2])
+            h_raw.append(h_tile)
+
+        load_h(0)
+        nu_raw = keep.tile([T_TILES, P], BF16, name="nu_raw")
+        nc.sync.dma_start(out=nu_raw[:], in_=nu.rearrange("(b p) -> b p", p=P))
+        for i in range(1, 4):
+            load_h(i)
+
+        def load_weight(words, scales, plane, name):
+            w_tile = keep.tile([P, K_PASSES, 2 * T], U8, name=name, align_bytes=64)
+            for q in range(4):
+                nc.sync.dma_start(
+                    out=plane[32 * q : 32 * q + 4, :, :].bitcast(I32),
+                    in_=scales[:, 4 * q : 4 * q + 4, :].rearrange("a r n -> r a n").bitcast(I32),
+                )
+            nc.sync.dma_start(out=w_tile[:].bitcast(I32), in_=words.rearrange("a p n -> p a n").bitcast(I32))
+            return w_tile
+
+        ws_w = load_weight(ws_words, ws_scales, ws_sc, "ws_w")
+        wm_w = load_weight(wm_words, wm_scales, wm_sc, "wm_w")
+
+        y_sb = []
+        e_sb = []
+        y_rows = y.rearrange("(g p j) t -> g p j t", g=GROUPS, j=PACK)
+        e_rows = e.rearrange("(g p j) m -> g p j m", g=GROUPS, j=PACK)
+        for gi in range(GROUPS):
+            y_tile = keep.tile([P, PACK, T], BF16, name="y_sb%d" % gi)
+            nc.sync.dma_start(out=y_tile[:], in_=y_rows[gi])
+            y_sb.append(y_tile)
+            e_tile = keep.tile([P, PACK, E], BF16, name="e_sb%d" % gi)
+            nc.sync.dma_start(out=e_tile[:], in_=e_rows[gi])
+            e_sb.append(e_tile)
+        g_raw = keep.tile([P, GROUPS, PACK], BF16, name="g_raw")
+        nc.sync.dma_start(out=g_raw[:], in_=g.rearrange("(g p j) -> p g j", g=GROUPS, j=PACK))
+
+        hs_all = keep.tile([P, P, 8], F32, name="hs_all")
+        nc.vector.tensor_copy(out=nu_rows[0:T_TILES, :], in_=nu_raw[:])
+        spread = [bank("spread0"), bank("spread1")]
+        for c in range(8):
+            nc.tensor.transpose(
+                spread[c // 4][:, P * (c % 4) : P * (c % 4 + 1)], hs_raw[:, c : c + 1].to_broadcast([P, P]), ident[:]
+            )
+        nu_bank = bank("nu_bank")
+        nc.tensor.transpose(nu_bank[:, 0:P], nu_rows[:], ident[:])
+        for half in range(2):
+            nc.vector.tensor_copy(
+                out=hs_all[:, :, 4 * half : 4 * half + 4], in_=spread[half][:].rearrange("q (c n) -> q n c", c=4)
+            )
+
+        nu_in = keep.tile([P, 2, T_TILES], F32, name="nu_in")
+        nu_inv = keep.tile([P, T_TILES], F32, name="nu_inv")
+        nu_log = keep.tile([P, 2, T_TILES], F32, name="nu_log")
+        root0 = keep.tile([P, T_TILES], F32, name="root0")
+        root_t = keep.tile([P, T_TILES], F32, name="root_t")
+        root = keep.tile([P, T_TILES], F32, name="root")
+        nc.vector.tensor_scalar(out=nu_in[:, 1, :], in0=nu_bank[:, 0:T_TILES], scalar1=1.0, scalar2=None, op0=ALU.add)
+        nc.vector.reciprocal(out=nu_inv[:], in_=nu_in[:, 1, :])
+        nc.vector.tensor_tensor(out=nu_in[:, 0, :], in0=nu_bank[:, 0:T_TILES], in1=nu_inv[:], op=ALU.mult)
+        nc.scalar.activation(out=nu_log[:], in_=nu_in[:], func=ACT.Ln)
+        nc.scalar.activation(out=root0[:], in_=nu_log[:, 1, :], func=ACT.Exp, scale=-0.5)
+
+        def polish_root():
+            nc.vector.tensor_tensor(out=root_t[:], in0=root0[:], in1=root0[:], op=ALU.mult)
+            nc.vector.tensor_tensor(out=root_t[:], in0=root_t[:], in1=nu_in[:, 1, :], op=ALU.mult)
+            nc.vector.tensor_scalar(
+                out=root_t[:], in0=root_t[:], scalar1=-0.5, scalar2=1.5, op0=ALU.mult, op1=ALU.add
+            )
+            nc.vector.tensor_tensor(out=root[:], in0=root0[:], in1=root_t[:], op=ALU.mult)
+
+        g_pos = keep.tile([P, GROUPS, PACK], F32, name="g_pos")
+        g_neg = keep.tile([P, GROUPS, PACK], F32, name="g_neg")
+
+        def widen_g():
+            nc.vector.tensor_copy(out=g_pos[:], in_=g_raw[:])
+            nc.vector.tensor_scalar(out=g_neg[:], in0=g_raw[:], scalar1=-1.0, scalar2=None, op0=ALU.mult)
+
+        h_codes = [keep.tile([P, K_PASSES, PASS], U32, name="h_codes%d" % gi, align_bytes=64) for gi in range(GROUPS)]
+        h_planes = [keep.tile([P, K_PASSES, PASS], U8, name="h_planes%d" % gi, align_bytes=64) for gi in range(GROUPS)]
+        h_wide = {}
+        h_turned = {}
+
+        def scale_h(i):
+            wide = work.tile([P, D], BF16, name="h_wide", tag="h_wide")
+            j = i % 2
+            nc.vector.tensor_tensor(
+                out=wide[:],
+                in0=h_raw[i // 2][:, D * j : D * (j + 1)].bitcast(FP8),
+                in1=hs_all[:].rearrange("q n c -> q (n c)"),
+                op=ALU.mult,
+            )
+            h_wide[i] = wide
+
+        def turn_h(i):
+            words = h_wide[i][:].bitcast(F32)
+            turned = bank("h_bank")
+            for a in range(K_PASSES):
+                for u in range(2):
+                    s = 2 * a + u
+                    nc.tensor.transpose(
+                        turned[:, P * s : P * (s + 1)], words[:, 256 * a + u : 256 * (a + 1) : 2], ident[:]
+                    )
+            grouped = work.tile([P, K_PASSES * P * PACK], BF16, name="h_grouped", tag="h_grouped", align_bytes=64)
+            nc.scalar.copy(
+                out=grouped[:].bitcast(F32).rearrange("p (a r u) -> p a r u", a=K_PASSES, u=2),
+                in_=turned[:].rearrange("p (a u r) -> p a r u", a=K_PASSES, u=2),
+            )
+            h_turned[i] = grouped
+
+        def quantise_h(i):
+            gi, j = divmod(i, PACK)
+            for a in range(K_PASSES):
+                nc.vector.quantize_mx(
+                    out=h_codes[gi][:, a, P * j : P * (j + 1)].bitcast(FP8X4),
+                    scales=h_planes[gi][:, a, P * j : P * (j + 1)],
+                    in_=h_turned[i][:, PASS * a : PASS * (a + 1)],
+                )
+
+        nq = {}
+
+        def log_precision(b, gi):
+            acc = bank("c_bank")
+            for a in range(K_PASSES):
+                nc.tensor.matmul_mx(
+                    out=acc[:],
+                    lhsT=ws_w[:, a, 2 * P * b : 2 * P * (b + 1)].bitcast(FP4X4),
+                    lhsT_scale=ws_sc[:, a, P * b : P * (b + 1)],
+                    rhs=h_codes[gi][:, a, :].bitcast(FP8X4),
+                    rhs_scale=h_planes[gi][:, a, :],
+                    start=(a == 0),
+                    stop=(a == K_PASSES - 1),
+                )
+            term = keep.tile([P, PASS], F32, name="nq%d_%d" % (b, gi))
+            nc.scalar.activation(out=term[:], in_=acc[:], func=ACT.Exp, scale=-2.0, bias=nu_log[:, 0, b : b + 1])
+            nq[b, gi] = term
+
+        e_codes = [keep.tile([P, E], U32, name="e_codes%d" % gi, align_bytes=64) for gi in range(GROUPS)]
+        e_planes = [keep.tile([P, E], U8, name="e_planes%d" % gi, align_bytes=64) for gi in range(GROUPS)]
+        e_grouped = [keep.tile([P, E, PACK], BF16, name="e_grouped%d" % gi, align_bytes=64) for gi in range(GROUPS)]
+
+        def interleave(dst, src):
+            nc.vector.tensor_copy(
+                out=dst[:].rearrange("p (c i) j -> p c j i", i=4), in_=src[:].rearrange("p j (c i) -> p c j i", i=4)
+            )
+
+        def quantise(codes, plane, grouped):
+            nc.vector.quantize_mx(
+                out=codes[:].bitcast(FP8X4), scales=plane[:], in_=grouped[:].rearrange("p c j -> p (c j)")
+            )
+
+        a_banks = {}
+        d_sb = {}
+        d2_sb = {}
+        dt_banks = {}
+        den_banks = {}
+        rs_sb = {}
+        u_sb = {}
+        grads = {}
+        grouped_grads = {}
+        quantised = {}
+        out_banks = {}
+
+        def location(c):
+            tq, gi = divmod(c, GROUPS)
+            a_banks[c] = []
+            for s in range(SUBS):
+                b = tq * SUBS + s
+                acc = bank("a_bank")
+                for j in range(PACK):
+                    for a in range(K_PASSES):
+                        nc.tensor.matmul_mx(
+                            out=acc[:, P * j : P * (j + 1)],
+                            lhsT=h_codes[gi][:, a, P * j : P * (j + 1)].bitcast(FP8X4),
+                            lhsT_scale=h_planes[gi][:, a, P * j : P * (j + 1)],
+                            rhs=wm_w[:, a, 2 * P * b : 2 * P * (b + 1)].bitcast(FP4X4),
+                            rhs_scale=wm_sc[:, a, P * b : P * (b + 1)],
+                            start=(a == 0),
+                            stop=(a == K_PASSES - 1),
+                        )
+                a_banks[c].append(acc)
+
+        def residual(c, s):
+            tq, gi = divmod(c, GROUPS)
+            if s == 0:
+                d_sb[c] = work.tile([P, PACK, W], F32, name="d_sb", tag="d_sb", bufs=4)
+            t0 = tq * W + s * P
+            nc.vector.tensor_tensor(
+                out=d_sb[c][:, :, P * s : P * (s + 1)],
+                in0=a_banks[c][s][:].rearrange("p (j t) -> p j t", j=PACK),
+                in1=y_sb[gi][:, :, t0 : t0 + P],
+                op=ALU.subtract,
+            )
+
+        def turn_residual(c):
+            dt_banks[c] = []
+            for s in range(SUBS):
+                turned = bank("dt_bank")
+                for j in range(PACK):
+                    nc.tensor.transpose(turned[:, P * j : P * (j + 1)], d_sb[c][:, j, P * s : P * (s + 1)], ident[:])
+                dt_banks[c].append(turned)
+
+        def square_residual(c):
+            tq = c // GROUPS
+            d2_sb[c] = []
+            for s in range(SUBS):
+                b = tq * SUBS + s
+                sq = work.tile([P, PASS], F32, name="d2_sb", tag="d2_sb", bufs=4)
+                nc.scalar.activation(out=sq[:], in_=dt_banks[c][s][:], func=ACT.Square, scale=root[:, b : b + 1])
+                d2_sb[c].append(sq)
+
+        def denominator(c):
+            tq, gi = divmod(c, GROUPS)
+            den_banks[c] = []
+            for s in range(SUBS):
+                b = tq * SUBS + s
+                acc = bank("den_bank")
+                for j in range(PACK):
+                    cols = slice(P * j, P * (j + 1))
+                    nc.tensor.matmul(
+                        acc[:, cols], lhsT=nq[b, gi][:, cols], rhs=ident[:], start=True, stop=False, is_transpose=True
+                    )
+                    nc.tensor.matmul(
+                        acc[:, cols], lhsT=d2_sb[c][s][:, cols], rhs=ident[:], start=False, stop=True, is_transpose=True
+                    )
+                den_banks[c].append(acc)
+
+        def inverse_root(c):
+            rs_sb[c] = work.tile([P, PACK, W], F32, name="rs_sb", tag="rs_sb")
+            for s in range(SUBS):
+                nc.scalar.activation(
+                    out=rs_sb[c][:, :, P * s : P * (s + 1)],
+                    in_=den_banks[c][s][:].rearrange("p (j t) -> p j t", j=PACK),
+                    func=ACT.Abs_reciprocal_sqrt,
+                )
+
+        def scaled_residual(c):
+            u_sb[c] = work.tile([P, PACK, W], F32, name="u_sb", tag="u_sb")
+            nc.vector.tensor_tensor(out=u_sb[c][:], in0=d_sb[c][:], in1=rs_sb[c][:], op=ALU.mult)
+
+        def grad_location(c):
+            gi = c % GROUPS
+            ga = work.tile([P, PACK, W], BF16, name="ga", tag="ga")
+            for j in range(PACK):
+                nc.vector.scalar_tensor_tensor(
+                    out=ga[:, j, :],
+                    in0=u_sb[c][:, j, :],
+                    scalar=g_pos[:, gi, j : j + 1],
+                    in1=rs_sb[c][:, j, :],
+                    op0=ALU.mult,
+                    op1=ALU.mult,
+                )
+            grads[0, c] = ga
+
+        def grad_precision(c):
+            gi = c % GROUPS
+            u2 = work.tile([P, PACK, W], F32, name="u2", tag="u2")
+            nc.scalar.activation(out=u2[:], in_=u_sb[c][:], func=ACT.Square)
+            gc = work.tile([P, PACK, W], BF16, name="gc", tag="gc")
+            for j in range(PACK):
+                nc.scalar.activation(
+                    out=gc[:, j, :],
+                    in_=u2[:, j, :],
+                    func=ACT.Identity,
+                    scale=g_pos[:, gi, j : j + 1],
+                    bias=g_neg[:, gi, j : j + 1],
+                )
+            grads[1, c] = gc
+
+        def group_grad(k, c):
+            grouped = work.tile([P, W, PACK], BF16, name="g_grouped", tag="g_grouped", align_bytes=64)
+            interleave(grouped, grads[k, c])
+            grouped_grads[k, c] = grouped
+
+        def quantise_grad(k, c):
+            codes = work.tile([P, W], U32, name="g_codes", tag="g_codes", bufs=6, align_bytes=64)
+            plane = work.tile([P, W], U8, name="g_plane", tag="g_plane", bufs=6, align_bytes=64)
+            quantise(codes, plane, grouped_grads[k, c])
+            quantised[k, c] = (codes, plane)
+
+        def contract(k, tq):
+            out_banks[k, tq] = []
+            for mp in range(E_TILES // 2):
+                acc = bank("out_bank")
+                for mm in range(2):
+                    m = 2 * mp + mm
+                    for gi in range(GROUPS):
+                        codes, plane = quantised[k, tq * GROUPS + gi]
+                        nc.tensor.matmul_mx(
+                            out=acc[:, W * mm : W * (mm + 1)],
+                            lhsT=e_codes[gi][:, P * m : P * (m + 1)].bitcast(FP8X4),
+                            lhsT_scale=e_planes[gi][:, P * m : P * (m + 1)],
+                            rhs=codes[:].bitcast(FP8X4),
+                            rhs_scale=plane[:],
+                            start=(gi == 0),
+                            stop=(gi == GROUPS - 1),
+                        )
+                out_banks[k, tq].append(acc)
+
+        def store(k, tq):
+            dst = (out_0, out_1)[k].rearrange("(mp mm p) t -> mp p mm t", mm=2, p=P)
+            for mp in range(E_TILES // 2):
+                result = work.tile([P, 2, W], F32, name="result", tag="result", bufs=4)
+                nc.scalar.activation(
+                    out=result[:],
+                    in_=out_banks[k, tq][mp][:].rearrange("p (mm t) -> p mm t", mm=2),
+                    func=ACT.Copy,
+                    scale=OUT_SCALE,
+                )
+                nc.sync.dma_start(out=dst[mp, :, :, tq * W : (tq + 1) * W], in_=result[:])
+
+        scale_h(0)
+        scale_h(1)
+        turn_h(0)
+        for i in range(2, 2 * PACK):
+            scale_h(i)
+            turn_h(i - 1)
+            quantise_h(i - 2)
+            if i >= 6:
+                for b in range(3 * (i - 6), 3 * (i - 5)):
+                    log_precision(b, 0)
+        turn_h(7)
+        quantise_h(6)
+        polish_root()
+        quantise_h(7)
+        widen_g()
+        log_precision(6, 0)
+        log_precision(7, 0)
+        location(0)
+        for s in range(SUBS):
+            residual(0, s)
+        for b in range(4):
+            log_precision(b, 1)
+        turn_residual(0)
+        square_residual(0)
+        for gi in range(GROUPS):
+            interleave(e_grouped[gi], e_sb[gi])
+        for gi in range(GROUPS):
+            quantise(e_codes[gi], e_planes[gi], e_grouped[gi])
+        for b in range(4, 8):
+            log_precision(b, 1)
+        denominator(0)
+        location(1)
+        for s in range(SUBS):
+            residual(1, s)
+        location(2)
+        turn_residual(1)
+        for s in range(SUBS):
+            residual(2, s)
+
+        def live(c):
+            return 0 <= c < CHUNKS
+
+        for i in range(1, CHUNKS + 3):
+            if live(i - 1):
+                inverse_root(i - 1)
+            if live(i + 2):
+                location(i + 2)
+            if i == 1:
+                square_residual(1)
+            if live(i - 2):
+                group_grad(0, i - 2)
+            if live(i + 2):
+                residual(i + 2, 0)
+            if live(i - 2):
+                quantise_grad(0, i - 2)
+            if live(i + 2):
+                residual(i + 2, 1)
+            k, tq = (i - 3) % 2, (i - 3) // 2
+            if i >= 3:
+                contract(k, tq)
+            if live(i - 1):
+                scaled_residual(i - 1)
+            if live(i - 2):
+                grad_precision(i - 2)
+            if live(i):
+                denominator(i)
+            if live(i + 1):
+                turn_residual(i + 1)
+            if live(i - 2):
+                group_grad(1, i - 2)
+            if live(i - 1):
+                grad_location(i - 1)
+            if live(i - 2):
+                quantise_grad(1, i - 2)
+            if i >= 3:
+                store(k, tq)
+            if live(i + 1):
+                square_residual(i + 1)

@@ -24,9 +24,12 @@ GROUPS = N // PASS
 K_PASSES = D // PASS
 T_TILES = T // P
 E_TILES = E // P
-W = 256
-SUBS = W // P
-CHUNKS = (T // W) * GROUPS
+WIDTHS = [128, 256, 256, 256, 128]
+STARTS = [sum(WIDTHS[:i]) for i in range(len(WIDTHS))]
+CHUNKS = len(WIDTHS) * GROUPS
+GC_ON_VECTOR = (4,9,)
+OUT_ON_VECTOR = (12,)
+WIDEN_ON_VECTOR = 2
 OUT_SCALE = 1.0 / 32.0
 
 
@@ -37,24 +40,30 @@ def tile_deeparstudentheadgradient_w4_kernel(
     with ExitStack() as ctx:
         keep = ctx.enter_context(tc.tile_pool(name="keep", bufs=1))
         work = ctx.enter_context(tc.tile_pool(name="work", bufs=3))
-        psum = ctx.enter_context(tc.psum_pool(name="psum", bufs=8))
+        psum = ctx.enter_context(tc.psum_pool(name="psum", bufs=1))
         ctx.enter_context(tc.manual_schedule())
 
-        def bank(name):
-            return psum.tile([P, PASS], F32, name=name, tag="bank")
+        free_banks = list(range(8))
+        bank_of = {}
 
-        ident = keep.tile([P, P], F32, name="ident")
-        make_identity(nc, ident[:])
-        nu_rows = keep.tile([P, P], F32, name="nu_rows")
-        nc.gpsimd.memset(nu_rows[:], 0.0)
+        def bank(*key):
+            slot = free_banks[0]
+            free_banks.remove(slot)
+            bank_of[key] = slot
+            return psum.tile([P, PASS], F32, name="%s_bank" % key[0], tag="bank%d" % slot)
+
+        def release(*key):
+            free_banks.append(bank_of[key])
 
         ws_sc = keep.tile([P, K_PASSES, T], U8, name="ws_sc", align_bytes=64)
         wm_sc = keep.tile([P, K_PASSES, T], U8, name="wm_sc", align_bytes=64)
+        nu_rows = keep.tile([P, 2, P], F32, name="nu_rows")
         nc.vector.memset(ws_sc[:].bitcast(I32), 0)
+        nc.vector.memset(nu_rows[:], 0.0)
         nc.vector.memset(wm_sc[:].bitcast(I32), 0)
+        ident = keep.tile([P, P], F32, name="ident")
+        make_identity(nc, ident[:])
 
-        hs_raw = keep.tile([P, 8], F32, name="hs_raw")
-        nc.sync.dma_start(out=hs_raw[:], in_=h_scale.rearrange("o (p c) -> p (o c)", c=8))
         h_rows = h_bytes.rearrange("(g p jj j) k -> g jj p (j k)", g=GROUPS, p=P, jj=2)
         h_raw = []
 
@@ -63,24 +72,31 @@ def tile_deeparstudentheadgradient_w4_kernel(
             nc.sync.dma_start(out=h_tile[:], in_=h_rows[i // 2, i % 2])
             h_raw.append(h_tile)
 
-        load_h(0)
-        nu_raw = keep.tile([T_TILES, P], BF16, name="nu_raw")
-        nc.sync.dma_start(out=nu_raw[:], in_=nu.rearrange("(b p) -> b p", p=P))
-        for i in range(1, 4):
-            load_h(i)
-
-        def load_weight(words, scales, plane, name):
-            w_tile = keep.tile([P, K_PASSES, 2 * T], U8, name=name, align_bytes=64)
+        def load_scales(queue, scales, plane):
             for q in range(4):
-                nc.sync.dma_start(
+                queue.dma_start(
                     out=plane[32 * q : 32 * q + 4, :, :].bitcast(I32),
                     in_=scales[:, 4 * q : 4 * q + 4, :].rearrange("a r n -> r a n").bitcast(I32),
                 )
+
+        def load_words(words, name):
+            w_tile = keep.tile([P, K_PASSES, 2 * T], U8, name=name, align_bytes=64)
             nc.sync.dma_start(out=w_tile[:].bitcast(I32), in_=words.rearrange("a p n -> p a n").bitcast(I32))
             return w_tile
 
-        ws_w = load_weight(ws_words, ws_scales, ws_sc, "ws_w")
-        wm_w = load_weight(wm_words, wm_scales, wm_sc, "wm_w")
+        nu_raw = keep.tile([T_TILES, P], BF16, name="nu_raw")
+        nc.sync.dma_start(out=nu_raw[:], in_=nu.rearrange("(b p) -> b p", p=P))
+        load_h(0)
+        hs_k = keep.tile([P, K_PASSES, PACK], F32, name="hs_k")
+        nc.sync.dma_start(out=hs_k[:], in_=h_scale.rearrange("o (a p j) -> p (o a) j", a=K_PASSES, j=PACK))
+        for i in range(1, 4):
+            load_h(i)
+        wm_w = load_words(wm_words, "wm_w")
+        g_raw = keep.tile([P, GROUPS, PACK], BF16, name="g_raw")
+        nc.sync.dma_start(out=g_raw[:], in_=g.rearrange("(g p j) -> p g j", g=GROUPS, j=PACK))
+        load_scales(nc.sync, wm_scales, wm_sc)
+        load_scales(nc.sync, ws_scales, ws_sc)
+        ws_w = load_words(ws_words, "ws_w")
 
         y_sb = []
         e_sb = []
@@ -93,42 +109,51 @@ def tile_deeparstudentheadgradient_w4_kernel(
             e_tile = keep.tile([P, PACK, E], BF16, name="e_sb%d" % gi)
             nc.sync.dma_start(out=e_tile[:], in_=e_rows[gi])
             e_sb.append(e_tile)
-        g_raw = keep.tile([P, GROUPS, PACK], BF16, name="g_raw")
-        nc.sync.dma_start(out=g_raw[:], in_=g.rearrange("(g p j) -> p g j", g=GROUPS, j=PACK))
 
-        hs_all = keep.tile([P, P, 8], F32, name="hs_all")
-        nc.vector.tensor_copy(out=nu_rows[0:T_TILES, :], in_=nu_raw[:])
-        spread = [bank("spread0"), bank("spread1")]
-        for c in range(8):
-            nc.tensor.transpose(
-                spread[c // 4][:, P * (c % 4) : P * (c % 4 + 1)], hs_raw[:, c : c + 1].to_broadcast([P, P]), ident[:]
-            )
-        nu_bank = bank("nu_bank")
-        nc.tensor.transpose(nu_bank[:, 0:P], nu_rows[:], ident[:])
-        for half in range(2):
-            nc.vector.tensor_copy(
-                out=hs_all[:, :, 4 * half : 4 * half + 4], in_=spread[half][:].rearrange("q (c n) -> q n c", c=4)
-            )
-
-        nu_in = keep.tile([P, 2, T_TILES], F32, name="nu_in")
+        nu_cols = keep.tile([P, 2, T_TILES], F32, name="nu_cols")
+        nu_one = keep.tile([P, T_TILES], F32, name="nu_one")
         nu_inv = keep.tile([P, T_TILES], F32, name="nu_inv")
-        nu_log = keep.tile([P, 2, T_TILES], F32, name="nu_log")
+        nu_ratio = keep.tile([P, T_TILES], F32, name="nu_ratio")
+        nu_log = keep.tile([P, T_TILES], F32, name="nu_log")
         root0 = keep.tile([P, T_TILES], F32, name="root0")
         root_t = keep.tile([P, T_TILES], F32, name="root_t")
         root = keep.tile([P, T_TILES], F32, name="root")
-        nc.vector.tensor_scalar(out=nu_in[:, 1, :], in0=nu_bank[:, 0:T_TILES], scalar1=1.0, scalar2=None, op0=ALU.add)
-        nc.vector.reciprocal(out=nu_inv[:], in_=nu_in[:, 1, :])
-        nc.vector.tensor_tensor(out=nu_in[:, 0, :], in0=nu_bank[:, 0:T_TILES], in1=nu_inv[:], op=ALU.mult)
-        nc.scalar.activation(out=nu_log[:], in_=nu_in[:], func=ACT.Ln)
-        nc.scalar.activation(out=root0[:], in_=nu_log[:, 1, :], func=ACT.Exp, scale=-0.5)
+        nc.scalar.activation(out=nu_rows[0:T_TILES, 1, :], in_=nu_raw[:], func=ACT.Ln, bias=1.0)
+        nc.vector.tensor_copy(out=nu_rows[0:T_TILES, 0, :], in_=nu_raw[:])
+        nu_bank = bank("nu")
+        for s in range(2):
+            nc.tensor.transpose(nu_bank[:, P * s : P * (s + 1)], nu_rows[:, s, :], ident[:])
 
-        def polish_root():
-            nc.vector.tensor_tensor(out=root_t[:], in0=root0[:], in1=root0[:], op=ALU.mult)
-            nc.vector.tensor_tensor(out=root_t[:], in0=root_t[:], in1=nu_in[:, 1, :], op=ALU.mult)
-            nc.vector.tensor_scalar(
-                out=root_t[:], in0=root_t[:], scalar1=-0.5, scalar2=1.5, op0=ALU.mult, op1=ALU.add
-            )
-            nc.vector.tensor_tensor(out=root[:], in0=root0[:], in1=root_t[:], op=ALU.mult)
+        def nu_step(s):
+            if s == 0:
+                turned = nu_bank[:, 0 : 2 * P].rearrange("p (s b) -> p s b", s=2)
+                nc.vector.tensor_copy(out=nu_cols[:], in_=turned[:, :, 0:T_TILES])
+                nc.vector.tensor_scalar(
+                    out=nu_one[:], in0=nu_bank[:, 0:T_TILES], scalar1=1.0, scalar2=None, op0=ALU.add
+                )
+                release("nu")
+            if s == 1:
+                nc.vector.reciprocal(out=nu_inv[:], in_=nu_one[:])
+            if s == 2:
+                nc.vector.tensor_tensor(out=nu_ratio[:], in0=nu_cols[:, 0, :], in1=nu_inv[:], op=ALU.mult)
+
+        def log_ratio():
+            nc.scalar.activation(out=nu_log[:], in_=nu_ratio[:], func=ACT.Ln)
+
+        def guess_root():
+            nc.scalar.activation(out=root0[:], in_=nu_cols[:, 1, :], func=ACT.Exp, scale=-0.5)
+
+        def polish_root(s):
+            if s == 0:
+                nc.vector.tensor_tensor(out=root_t[:], in0=root0[:], in1=root0[:], op=ALU.mult)
+            if s == 1:
+                nc.vector.scalar_tensor_tensor(
+                    out=root_t[:], in0=root_t[:], scalar=-0.5, in1=nu_one[:], op0=ALU.mult, op1=ALU.mult
+                )
+            if s == 2:
+                nc.vector.scalar_tensor_tensor(
+                    out=root[:], in0=root_t[:], scalar=1.5, in1=root0[:], op0=ALU.add, op1=ALU.mult
+                )
 
         g_pos = keep.tile([P, GROUPS, PACK], F32, name="g_pos")
         g_neg = keep.tile([P, GROUPS, PACK], F32, name="g_neg")
@@ -141,32 +166,39 @@ def tile_deeparstudentheadgradient_w4_kernel(
         h_planes = [keep.tile([P, K_PASSES, PASS], U8, name="h_planes%d" % gi, align_bytes=64) for gi in range(GROUPS)]
         h_wide = {}
         h_turned = {}
+        h_banks = {}
 
-        def scale_h(i):
-            wide = work.tile([P, D], BF16, name="h_wide", tag="h_wide")
+        def widen_h(i):
+            wide = work.tile([P, D], BF16, name="h_wide", tag="h_wide", bufs=4)
             j = i % 2
-            nc.vector.tensor_tensor(
-                out=wide[:],
-                in0=h_raw[i // 2][:, D * j : D * (j + 1)].bitcast(FP8),
-                in1=hs_all[:].rearrange("q n c -> q (n c)"),
-                op=ALU.mult,
-            )
+            codes = h_raw[i // 2][:, D * j : D * (j + 1)].bitcast(FP8)
+            if i < WIDEN_ON_VECTOR:
+                nc.vector.tensor_copy(out=wide[:], in_=codes)
+            else:
+                nc.scalar.copy(out=wide[:], in_=codes)
             h_wide[i] = wide
 
         def turn_h(i):
             words = h_wide[i][:].bitcast(F32)
-            turned = bank("h_bank")
+            turned = bank("h", i)
             for a in range(K_PASSES):
                 for u in range(2):
                     s = 2 * a + u
                     nc.tensor.transpose(
                         turned[:, P * s : P * (s + 1)], words[:, 256 * a + u : 256 * (a + 1) : 2], ident[:]
                     )
+            h_banks[i] = turned
+
+        def scale_h(i):
             grouped = work.tile([P, K_PASSES * P * PACK], BF16, name="h_grouped", tag="h_grouped", align_bytes=64)
-            nc.scalar.copy(
-                out=grouped[:].bitcast(F32).rearrange("p (a r u) -> p a r u", a=K_PASSES, u=2),
-                in_=turned[:].rearrange("p (a u r) -> p a r u", a=K_PASSES, u=2),
-            )
+            for a in range(K_PASSES):
+                nc.vector.tensor_tensor(
+                    out=grouped[:, PASS * a : PASS * (a + 1)].rearrange("p (r u v) -> p r u v", u=2, v=2),
+                    in0=h_banks[i][:, 256 * a : 256 * (a + 1)].bitcast(BF16).rearrange("p (u r v) -> p r u v", u=2, v=2),
+                    in1=hs_k[:, a, :].rearrange("p (u v) -> p u v", u=2).unsqueeze(1).to_broadcast([P, P, 2, 2]),
+                    op=ALU.mult,
+                )
+            release("h", i)
             h_turned[i] = grouped
 
         def quantise_h(i):
@@ -181,7 +213,7 @@ def tile_deeparstudentheadgradient_w4_kernel(
         nq = {}
 
         def log_precision(b, gi):
-            acc = bank("c_bank")
+            acc = bank("c", b, gi)
             for a in range(K_PASSES):
                 nc.tensor.matmul_mx(
                     out=acc[:],
@@ -193,7 +225,8 @@ def tile_deeparstudentheadgradient_w4_kernel(
                     stop=(a == K_PASSES - 1),
                 )
             term = keep.tile([P, PASS], F32, name="nq%d_%d" % (b, gi))
-            nc.scalar.activation(out=term[:], in_=acc[:], func=ACT.Exp, scale=-2.0, bias=nu_log[:, 0, b : b + 1])
+            nc.scalar.activation(out=term[:], in_=acc[:], func=ACT.Exp, scale=-2.0, bias=nu_log[:, b : b + 1])
+            release("c", b, gi)
             nq[b, gi] = term
 
         e_codes = [keep.tile([P, E], U32, name="e_codes%d" % gi, align_bytes=64) for gi in range(GROUPS)]
@@ -217,18 +250,25 @@ def tile_deeparstudentheadgradient_w4_kernel(
         den_banks = {}
         rs_sb = {}
         u_sb = {}
+        u2_sb = {}
         grads = {}
         grouped_grads = {}
         quantised = {}
         out_banks = {}
 
-        def location(c):
-            tq, gi = divmod(c, GROUPS)
-            a_banks[c] = []
-            for s in range(SUBS):
-                b = tq * SUBS + s
-                acc = bank("a_bank")
-                for j in range(PACK):
+        def tiles_of(c):
+            blk = c // GROUPS
+            return range(STARTS[blk] // P, (STARTS[blk] + WIDTHS[blk]) // P)
+
+        def width(c):
+            return WIDTHS[c // GROUPS]
+
+        def location(c, rows=range(PACK)):
+            gi = c % GROUPS
+            if 0 in rows:
+                a_banks[c] = [bank("a", b, gi) for b in tiles_of(c)]
+            for acc, b in zip(a_banks[c], tiles_of(c)):
+                for j in rows:
                     for a in range(K_PASSES):
                         nc.tensor.matmul_mx(
                             out=acc[:, P * j : P * (j + 1)],
@@ -239,43 +279,43 @@ def tile_deeparstudentheadgradient_w4_kernel(
                             start=(a == 0),
                             stop=(a == K_PASSES - 1),
                         )
-                a_banks[c].append(acc)
 
         def residual(c, s):
-            tq, gi = divmod(c, GROUPS)
+            gi = c % GROUPS
+            if s >= len(tiles_of(c)):
+                return
             if s == 0:
-                d_sb[c] = work.tile([P, PACK, W], F32, name="d_sb", tag="d_sb", bufs=4)
-            t0 = tq * W + s * P
+                d_sb[c] = work.tile([P, PACK, width(c)], F32, name="d_sb", tag="d_sb", bufs=6)
+            b = tiles_of(c)[s]
             nc.vector.tensor_tensor(
                 out=d_sb[c][:, :, P * s : P * (s + 1)],
                 in0=a_banks[c][s][:].rearrange("p (j t) -> p j t", j=PACK),
-                in1=y_sb[gi][:, :, t0 : t0 + P],
+                in1=y_sb[gi][:, :, P * b : P * (b + 1)],
                 op=ALU.subtract,
             )
+            release("a", b, gi)
 
         def turn_residual(c):
             dt_banks[c] = []
-            for s in range(SUBS):
-                turned = bank("dt_bank")
+            for s in range(len(tiles_of(c))):
+                turned = bank("dt", c, s)
                 for j in range(PACK):
                     nc.tensor.transpose(turned[:, P * j : P * (j + 1)], d_sb[c][:, j, P * s : P * (s + 1)], ident[:])
                 dt_banks[c].append(turned)
 
         def square_residual(c):
-            tq = c // GROUPS
             d2_sb[c] = []
-            for s in range(SUBS):
-                b = tq * SUBS + s
+            for s, b in enumerate(tiles_of(c)):
                 sq = work.tile([P, PASS], F32, name="d2_sb", tag="d2_sb", bufs=4)
                 nc.scalar.activation(out=sq[:], in_=dt_banks[c][s][:], func=ACT.Square, scale=root[:, b : b + 1])
+                release("dt", c, s)
                 d2_sb[c].append(sq)
 
         def denominator(c):
-            tq, gi = divmod(c, GROUPS)
+            gi = c % GROUPS
             den_banks[c] = []
-            for s in range(SUBS):
-                b = tq * SUBS + s
-                acc = bank("den_bank")
+            for s, b in enumerate(tiles_of(c)):
+                acc = bank("den", c, s)
                 for j in range(PACK):
                     cols = slice(P * j, P * (j + 1))
                     nc.tensor.matmul(
@@ -287,21 +327,22 @@ def tile_deeparstudentheadgradient_w4_kernel(
                 den_banks[c].append(acc)
 
         def inverse_root(c):
-            rs_sb[c] = work.tile([P, PACK, W], F32, name="rs_sb", tag="rs_sb")
-            for s in range(SUBS):
+            rs_sb[c] = work.tile([P, PACK, width(c)], F32, name="rs_sb", tag="rs_sb")
+            for s in range(len(tiles_of(c))):
                 nc.scalar.activation(
                     out=rs_sb[c][:, :, P * s : P * (s + 1)],
                     in_=den_banks[c][s][:].rearrange("p (j t) -> p j t", j=PACK),
                     func=ACT.Abs_reciprocal_sqrt,
                 )
+                release("den", c, s)
 
         def scaled_residual(c):
-            u_sb[c] = work.tile([P, PACK, W], F32, name="u_sb", tag="u_sb")
+            u_sb[c] = work.tile([P, PACK, width(c)], F32, name="u_sb", tag="u_sb")
             nc.vector.tensor_tensor(out=u_sb[c][:], in0=d_sb[c][:], in1=rs_sb[c][:], op=ALU.mult)
 
         def grad_location(c):
             gi = c % GROUPS
-            ga = work.tile([P, PACK, W], BF16, name="ga", tag="ga")
+            ga = work.tile([P, PACK, width(c)], BF16, name="ga", tag="ga")
             for j in range(PACK):
                 nc.vector.scalar_tensor_tensor(
                     out=ga[:, j, :],
@@ -313,42 +354,59 @@ def tile_deeparstudentheadgradient_w4_kernel(
                 )
             grads[0, c] = ga
 
-        def grad_precision(c):
+        def square_scaled(c):
+            u2 = work.tile([P, PACK, width(c)], F32, name="u2", tag="u2")
+            for half in range(2):
+                rows = slice(2 * half, 2 * half + 2)
+                nc.scalar.activation(out=u2[:, rows, :], in_=u_sb[c][:, rows, :], func=ACT.Square)
+            u2_sb[c] = u2
+
+        def grad_precision(c, on_vector):
             gi = c % GROUPS
-            u2 = work.tile([P, PACK, W], F32, name="u2", tag="u2")
-            nc.scalar.activation(out=u2[:], in_=u_sb[c][:], func=ACT.Square)
-            gc = work.tile([P, PACK, W], BF16, name="gc", tag="gc")
+            gc = work.tile([P, PACK, width(c)], BF16, name="gc", tag="gc")
             for j in range(PACK):
-                nc.scalar.activation(
-                    out=gc[:, j, :],
-                    in_=u2[:, j, :],
-                    func=ACT.Identity,
-                    scale=g_pos[:, gi, j : j + 1],
-                    bias=g_neg[:, gi, j : j + 1],
-                )
+                if on_vector:
+                    nc.vector.tensor_scalar(
+                        out=gc[:, j, :],
+                        in0=u2_sb[c][:, j, :],
+                        scalar1=g_pos[:, gi, j : j + 1],
+                        scalar2=g_neg[:, gi, j : j + 1],
+                        op0=ALU.mult,
+                        op1=ALU.add,
+                    )
+                else:
+                    nc.scalar.activation(
+                        out=gc[:, j, :],
+                        in_=u2_sb[c][:, j, :],
+                        func=ACT.Identity,
+                        scale=g_pos[:, gi, j : j + 1],
+                        bias=g_neg[:, gi, j : j + 1],
+                    )
             grads[1, c] = gc
 
         def group_grad(k, c):
-            grouped = work.tile([P, W, PACK], BF16, name="g_grouped", tag="g_grouped", align_bytes=64)
+            grouped = work.tile([P, width(c), PACK], BF16, name="g_grouped", tag="g_grouped", align_bytes=64)
             interleave(grouped, grads[k, c])
             grouped_grads[k, c] = grouped
 
         def quantise_grad(k, c):
-            codes = work.tile([P, W], U32, name="g_codes", tag="g_codes", bufs=6, align_bytes=64)
-            plane = work.tile([P, W], U8, name="g_plane", tag="g_plane", bufs=6, align_bytes=64)
+            codes = work.tile([P, width(c)], U32, name="g_codes", tag="g_codes", bufs=8, align_bytes=64)
+            plane = work.tile([P, width(c)], U8, name="g_plane", tag="g_plane", bufs=8, align_bytes=64)
             quantise(codes, plane, grouped_grads[k, c])
             quantised[k, c] = (codes, plane)
 
-        def contract(k, tq):
-            out_banks[k, tq] = []
-            for mp in range(E_TILES // 2):
-                acc = bank("out_bank")
-                for mm in range(2):
-                    m = 2 * mp + mm
+        def contract(k, blk):
+            w = WIDTHS[blk]
+            per_bank = PASS // w
+            out_banks[k, blk] = []
+            for mp in range(E_TILES // per_bank):
+                acc = bank("out", k, blk, mp)
+                for mm in range(per_bank):
+                    m = per_bank * mp + mm
                     for gi in range(GROUPS):
-                        codes, plane = quantised[k, tq * GROUPS + gi]
+                        codes, plane = quantised[k, blk * GROUPS + gi]
                         nc.tensor.matmul_mx(
-                            out=acc[:, W * mm : W * (mm + 1)],
+                            out=acc[:, w * mm : w * (mm + 1)],
                             lhsT=e_codes[gi][:, P * m : P * (m + 1)].bitcast(FP8X4),
                             lhsT_scale=e_planes[gi][:, P * m : P * (m + 1)],
                             rhs=codes[:].bitcast(FP8X4),
@@ -356,41 +414,57 @@ def tile_deeparstudentheadgradient_w4_kernel(
                             start=(gi == 0),
                             stop=(gi == GROUPS - 1),
                         )
-                out_banks[k, tq].append(acc)
+                out_banks[k, blk].append(acc)
 
-        def store(k, tq):
-            dst = (out_0, out_1)[k].rearrange("(mp mm p) t -> mp p mm t", mm=2, p=P)
-            for mp in range(E_TILES // 2):
-                result = work.tile([P, 2, W], F32, name="result", tag="result", bufs=4)
-                nc.scalar.activation(
-                    out=result[:],
-                    in_=out_banks[k, tq][mp][:].rearrange("p (mm t) -> p mm t", mm=2),
-                    func=ACT.Copy,
-                    scale=OUT_SCALE,
-                )
-                nc.sync.dma_start(out=dst[mp, :, :, tq * W : (tq + 1) * W], in_=result[:])
+        def store(k, blk, on_vector):
+            w = WIDTHS[blk]
+            per_bank = PASS // w
+            dst = (out_0, out_1)[k].rearrange("(mp mm p) t -> mp p mm t", mm=per_bank, p=P)
+            for mp in range(E_TILES // per_bank):
+                result = work.tile([P, per_bank, w], F32, name="result", tag="result", bufs=6)
+                sums = out_banks[k, blk][mp][:].rearrange("p (mm t) -> p mm t", mm=per_bank)
+                if on_vector:
+                    nc.vector.tensor_scalar(out=result[:], in0=sums, scalar1=OUT_SCALE, scalar2=None, op0=ALU.mult)
+                else:
+                    nc.scalar.activation(out=result[:], in_=sums, func=ACT.Copy, scale=OUT_SCALE)
+                release("out", k, blk, mp)
+                nc.sync.dma_start(out=dst[mp, :, :, STARTS[blk] : STARTS[blk] + w], in_=result[:])
 
-        scale_h(0)
-        scale_h(1)
+        tiles = GROUPS * PACK
+        widen_h(0)
         turn_h(0)
-        for i in range(2, 2 * PACK):
+        nu_step(0)
+        widen_h(1)
+        nu_step(1)
+        turn_h(1)
+        widen_h(2)
+        for i in range(tiles):
+            if i + 3 < tiles:
+                widen_h(i + 3)
+            if i + 2 < tiles:
+                turn_h(i + 2)
             scale_h(i)
-            turn_h(i - 1)
-            quantise_h(i - 2)
-            if i >= 6:
-                for b in range(3 * (i - 6), 3 * (i - 5)):
+            if i == 0:
+                nu_step(2)
+                log_ratio()
+            if i >= 1:
+                quantise_h(i - 1)
+            if 1 <= i <= PACK:
+                location(0, [i - 1])
+                location(2, [i - 1])
+            if i == 4:
+                guess_root()
+            if i >= 5:
+                polish_root(i - 5)
+            if i >= 4:
+                for b in range(2 * (i - 4), 2 * (i - 3)):
                     log_precision(b, 0)
-        turn_h(7)
-        quantise_h(6)
-        polish_root()
-        quantise_h(7)
         widen_g()
-        log_precision(6, 0)
-        log_precision(7, 0)
-        location(0)
-        for s in range(SUBS):
-            residual(0, s)
-        for b in range(4):
+        quantise_h(tiles - 1)
+        residual(0, 0)
+        for s in range(2):
+            residual(2, s)
+        for b in range(3):
             log_precision(b, 1)
         turn_residual(0)
         square_residual(0)
@@ -398,53 +472,57 @@ def tile_deeparstudentheadgradient_w4_kernel(
             interleave(e_grouped[gi], e_sb[gi])
         for gi in range(GROUPS):
             quantise(e_codes[gi], e_planes[gi], e_grouped[gi])
-        for b in range(4, 8):
+        for b in range(3, T_TILES):
             log_precision(b, 1)
-        denominator(0)
         location(1)
-        for s in range(SUBS):
-            residual(1, s)
-        location(2)
+        residual(1, 0)
+        denominator(0)
+        turn_residual(2)
         turn_residual(1)
-        for s in range(SUBS):
-            residual(2, s)
 
         def live(c):
             return 0 <= c < CHUNKS
 
-        for i in range(1, CHUNKS + 3):
+        def late(c):
+            return live(c) and c != 2
+
+        for i in range(1, CHUNKS + 4):
             if live(i - 1):
                 inverse_root(i - 1)
-            if live(i + 2):
-                location(i + 2)
+            if late(i + 1):
+                location(i + 1)
             if i == 1:
                 square_residual(1)
+            if live(i - 3):
+                group_grad(1, i - 3)
             if live(i - 2):
                 group_grad(0, i - 2)
-            if live(i + 2):
-                residual(i + 2, 0)
-            if live(i - 2):
-                quantise_grad(0, i - 2)
-            if live(i + 2):
-                residual(i + 2, 1)
-            k, tq = (i - 3) % 2, (i - 3) // 2
-            if i >= 3:
-                contract(k, tq)
+            if live(i - 3):
+                quantise_grad(1, i - 3)
+            if late(i + 1):
+                residual(i + 1, 0)
+            if late(i + 1):
+                residual(i + 1, 1)
             if live(i - 1):
                 scaled_residual(i - 1)
             if live(i - 2):
-                grad_precision(i - 2)
-            if live(i):
-                denominator(i)
-            if live(i + 1):
-                turn_residual(i + 1)
+                quantise_grad(0, i - 2)
+            k, blk = (i - 4) % 2, (i - 4) // 2
+            if i >= 4:
+                contract(k, blk)
             if live(i - 2):
-                group_grad(1, i - 2)
+                square_scaled(i - 2)
+            if live(i - 2) and (i - 2) in GC_ON_VECTOR:
+                grad_precision(i - 2, True)
             if live(i - 1):
                 grad_location(i - 1)
-            if live(i - 2):
-                quantise_grad(1, i - 2)
-            if i >= 3:
-                store(k, tq)
+            if live(i - 2) and (i - 2) not in GC_ON_VECTOR:
+                grad_precision(i - 2, False)
+            if live(i):
+                denominator(i)
+            if late(i + 1):
+                turn_residual(i + 1)
+            if i >= 4:
+                store(k, blk, i in OUT_ON_VECTOR)
             if live(i + 1):
                 square_residual(i + 1)

@@ -24,11 +24,11 @@ GROUPS = N // PASS
 K_PASSES = D // PASS
 T_TILES = T // P
 E_TILES = E // P
-WIDTHS = [128, 256, 256, 256, 128]
+WIDTHS = [256, 256, 256, 256]
 STARTS = [sum(WIDTHS[:i]) for i in range(len(WIDTHS))]
 CHUNKS = len(WIDTHS) * GROUPS
-GC_ON_VECTOR = (4,9,)
-OUT_ON_VECTOR = (12,)
+GC_ON_VECTOR = (4,)
+OUT_ON_VECTOR = ()
 WIDEN_ON_VECTOR = 2
 OUT_SCALE = 1.0 / 32.0
 
@@ -91,12 +91,12 @@ def tile_deeparstudentheadgradient_w4_kernel(
         nc.sync.dma_start(out=hs_k[:], in_=h_scale.rearrange("o (a p j) -> p (o a) j", a=K_PASSES, j=PACK))
         for i in range(1, 4):
             load_h(i)
-        wm_w = load_words(wm_words, "wm_w")
+        ws_w = load_words(ws_words, "ws_w")
         g_raw = keep.tile([P, GROUPS, PACK], BF16, name="g_raw")
         nc.sync.dma_start(out=g_raw[:], in_=g.rearrange("(g p j) -> p g j", g=GROUPS, j=PACK))
-        load_scales(nc.sync, wm_scales, wm_sc)
         load_scales(nc.sync, ws_scales, ws_sc)
-        ws_w = load_words(ws_words, "ws_w")
+        load_scales(nc.sync, wm_scales, wm_sc)
+        wm_w = load_words(wm_words, "wm_w")
 
         y_sb = []
         e_sb = []
@@ -183,32 +183,33 @@ def tile_deeparstudentheadgradient_w4_kernel(
             turned = bank("h", i)
             for a in range(K_PASSES):
                 for u in range(2):
-                    s = 2 * a + u
+                    s = K_PASSES * u + a
                     nc.tensor.transpose(
                         turned[:, P * s : P * (s + 1)], words[:, 256 * a + u : 256 * (a + 1) : 2], ident[:]
                     )
             h_banks[i] = turned
 
         def scale_h(i):
-            grouped = work.tile([P, K_PASSES * P * PACK], BF16, name="h_grouped", tag="h_grouped", align_bytes=64)
-            for a in range(K_PASSES):
-                nc.vector.tensor_tensor(
-                    out=grouped[:, PASS * a : PASS * (a + 1)].rearrange("p (r u v) -> p r u v", u=2, v=2),
-                    in0=h_banks[i][:, 256 * a : 256 * (a + 1)].bitcast(BF16).rearrange("p (u r v) -> p r u v", u=2, v=2),
-                    in1=hs_k[:, a, :].rearrange("p (u v) -> p u v", u=2).unsqueeze(1).to_broadcast([P, P, 2, 2]),
-                    op=ALU.mult,
+            if i % 2 == 0:
+                h_turned[i // 2] = work.tile(
+                    [P, K_PASSES, 2, P * PACK], BF16, name="h_grouped", tag="h_grouped", bufs=2, align_bytes=64
                 )
+            nc.vector.tensor_tensor(
+                out=h_turned[i // 2][:, :, i % 2, :].rearrange("p a (r u v) -> p a r u v", u=2, v=2),
+                in0=h_banks[i][:].bitcast(BF16).rearrange("p (u a r v) -> p a r u v", u=2, a=K_PASSES, v=2),
+                in1=hs_k[:].rearrange("p a (u v) -> p a u v", u=2).unsqueeze(2).to_broadcast([P, K_PASSES, P, 2, 2]),
+                op=ALU.mult,
+            )
             release("h", i)
-            h_turned[i] = grouped
 
-        def quantise_h(i):
-            gi, j = divmod(i, PACK)
-            for a in range(K_PASSES):
-                nc.vector.quantize_mx(
-                    out=h_codes[gi][:, a, P * j : P * (j + 1)].bitcast(FP8X4),
-                    scales=h_planes[gi][:, a, P * j : P * (j + 1)],
-                    in_=h_turned[i][:, PASS * a : PASS * (a + 1)],
-                )
+        def quantise_h(pair, a):
+            gi, jj = divmod(pair, 2)
+            cols = slice(2 * P * jj, 2 * P * (jj + 1))
+            nc.vector.quantize_mx(
+                out=h_codes[gi][:, a, cols].bitcast(FP8X4),
+                scales=h_planes[gi][:, a, cols],
+                in_=h_turned[pair][:, a, :, :].rearrange("p j x -> p (j x)"),
+            )
 
         nq = {}
 
@@ -285,7 +286,7 @@ def tile_deeparstudentheadgradient_w4_kernel(
             if s >= len(tiles_of(c)):
                 return
             if s == 0:
-                d_sb[c] = work.tile([P, PACK, width(c)], F32, name="d_sb", tag="d_sb", bufs=6)
+                d_sb[c] = work.tile([P, PACK, width(c)], F32, name="d_sb", tag="d_sb", bufs=4)
             b = tiles_of(c)[s]
             nc.vector.tensor_tensor(
                 out=d_sb[c][:, :, P * s : P * (s + 1)],
@@ -340,34 +341,35 @@ def tile_deeparstudentheadgradient_w4_kernel(
             u_sb[c] = work.tile([P, PACK, width(c)], F32, name="u_sb", tag="u_sb")
             nc.vector.tensor_tensor(out=u_sb[c][:], in0=d_sb[c][:], in1=rs_sb[c][:], op=ALU.mult)
 
+        def open_pair(s):
+            if s not in grads:
+                grads[s] = work.tile([P, 2, PACK, WIDTHS[0]], BF16, name="grads", tag="grads")
+
         def grad_location(c):
             gi = c % GROUPS
-            ga = work.tile([P, PACK, width(c)], BF16, name="ga", tag="ga")
+            open_pair(c)
             for j in range(PACK):
                 nc.vector.scalar_tensor_tensor(
-                    out=ga[:, j, :],
+                    out=grads[c][:, 0, j, :],
                     in0=u_sb[c][:, j, :],
                     scalar=g_pos[:, gi, j : j + 1],
                     in1=rs_sb[c][:, j, :],
                     op0=ALU.mult,
                     op1=ALU.mult,
                 )
-            grads[0, c] = ga
 
         def square_scaled(c):
             u2 = work.tile([P, PACK, width(c)], F32, name="u2", tag="u2")
-            for half in range(2):
-                rows = slice(2 * half, 2 * half + 2)
-                nc.scalar.activation(out=u2[:, rows, :], in_=u_sb[c][:, rows, :], func=ACT.Square)
+            nc.scalar.activation(out=u2[:], in_=u_sb[c][:], func=ACT.Square)
             u2_sb[c] = u2
 
         def grad_precision(c, on_vector):
             gi = c % GROUPS
-            gc = work.tile([P, PACK, width(c)], BF16, name="gc", tag="gc")
+            open_pair(c + 1)
             for j in range(PACK):
                 if on_vector:
                     nc.vector.tensor_scalar(
-                        out=gc[:, j, :],
+                        out=grads[c + 1][:, 1, j, :],
                         in0=u2_sb[c][:, j, :],
                         scalar1=g_pos[:, gi, j : j + 1],
                         scalar2=g_neg[:, gi, j : j + 1],
@@ -376,24 +378,33 @@ def tile_deeparstudentheadgradient_w4_kernel(
                     )
                 else:
                     nc.scalar.activation(
-                        out=gc[:, j, :],
+                        out=grads[c + 1][:, 1, j, :],
                         in_=u2_sb[c][:, j, :],
                         func=ACT.Identity,
                         scale=g_pos[:, gi, j : j + 1],
                         bias=g_neg[:, gi, j : j + 1],
                     )
-            grads[1, c] = gc
 
-        def group_grad(k, c):
-            grouped = work.tile([P, width(c), PACK], BF16, name="g_grouped", tag="g_grouped", align_bytes=64)
-            interleave(grouped, grads[k, c])
-            grouped_grads[k, c] = grouped
+        def group_grads(c, ks):
+            grouped = work.tile(
+                [P, len(ks), WIDTHS[0], PACK], BF16, name="g_grouped", tag="g_grouped", bufs=3, align_bytes=64
+            )
+            nc.vector.tensor_copy(
+                out=grouped[:].rearrange("p k (c i) j -> p k c j i", i=4),
+                in_=grads[c][:, ks[0] : ks[-1] + 1, :, :].rearrange("p k j (c i) -> p k c j i", i=4),
+            )
+            grouped_grads[c, ks] = grouped
 
-        def quantise_grad(k, c):
-            codes = work.tile([P, width(c)], U32, name="g_codes", tag="g_codes", bufs=8, align_bytes=64)
-            plane = work.tile([P, width(c)], U8, name="g_plane", tag="g_plane", bufs=8, align_bytes=64)
-            quantise(codes, plane, grouped_grads[k, c])
-            quantised[k, c] = (codes, plane)
+        def quantise_grads(c, ks):
+            codes = work.tile([P, len(ks), WIDTHS[0]], U32, name="g_codes", tag="g_codes", bufs=5, align_bytes=64)
+            plane = work.tile([P, len(ks), WIDTHS[0]], U8, name="g_plane", tag="g_plane", bufs=5, align_bytes=64)
+            nc.vector.quantize_mx(
+                out=codes[:].rearrange("p k t -> p (k t)").bitcast(FP8X4),
+                scales=plane[:].rearrange("p k t -> p (k t)"),
+                in_=grouped_grads[c, ks][:].rearrange("p k t j -> p (k t j)"),
+            )
+            for s, k in enumerate(ks):
+                quantised[k, c - k] = (codes[:, s, :], plane[:, s, :])
 
         def contract(k, blk):
             w = WIDTHS[blk]
@@ -409,18 +420,20 @@ def tile_deeparstudentheadgradient_w4_kernel(
                             out=acc[:, w * mm : w * (mm + 1)],
                             lhsT=e_codes[gi][:, P * m : P * (m + 1)].bitcast(FP8X4),
                             lhsT_scale=e_planes[gi][:, P * m : P * (m + 1)],
-                            rhs=codes[:].bitcast(FP8X4),
-                            rhs_scale=plane[:],
+                            rhs=codes.bitcast(FP8X4),
+                            rhs_scale=plane,
                             start=(gi == 0),
                             stop=(gi == GROUPS - 1),
                         )
                 out_banks[k, blk].append(acc)
 
-        def store(k, blk, on_vector):
+        def store(k, blk, on_vector, only=None):
             w = WIDTHS[blk]
             per_bank = PASS // w
             dst = (out_0, out_1)[k].rearrange("(mp mm p) t -> mp p mm t", mm=per_bank, p=P)
             for mp in range(E_TILES // per_bank):
+                if only is not None and mp % 2 != only:
+                    continue
                 result = work.tile([P, per_bank, w], F32, name="result", tag="result", bufs=6)
                 sums = out_banks[k, blk][mp][:].rearrange("p (mm t) -> p mm t", mm=per_bank)
                 if on_vector:
@@ -441,29 +454,28 @@ def tile_deeparstudentheadgradient_w4_kernel(
         for i in range(tiles):
             if i + 3 < tiles:
                 widen_h(i + 3)
-            if i + 2 < tiles:
+            if i + 2 < tiles and i < PACK:
                 turn_h(i + 2)
+            if i == PACK:
+                turn_h(6)
+                turn_h(7)
+                guess_root()
+                for b in range(T_TILES):
+                    log_precision(b, 0)
+                location(0)
             scale_h(i)
             if i == 0:
                 nu_step(2)
                 log_ratio()
-            if i >= 1:
-                quantise_h(i - 1)
-            if 1 <= i <= PACK:
-                location(0, [i - 1])
-                location(2, [i - 1])
-            if i == 4:
-                guess_root()
-            if i >= 5:
-                polish_root(i - 5)
-            if i >= 4:
-                for b in range(2 * (i - 4), 2 * (i - 3)):
-                    log_precision(b, 0)
-        widen_g()
-        quantise_h(tiles - 1)
-        residual(0, 0)
+            if i > PACK:
+                polish_root(i - PACK - 1)
+            if i == tiles - 1:
+                widen_g()
+            if i % PACK >= 2:
+                for a in range(K_PASSES):
+                    quantise_h(i // 2 - 1 + i % 2, a)
         for s in range(2):
-            residual(2, s)
+            residual(0, s)
         for b in range(3):
             log_precision(b, 1)
         turn_residual(0)
@@ -475,10 +487,14 @@ def tile_deeparstudentheadgradient_w4_kernel(
         for b in range(3, T_TILES):
             log_precision(b, 1)
         location(1)
-        residual(1, 0)
+        for s in range(2):
+            residual(1, s)
         denominator(0)
-        turn_residual(2)
+        location(2)
+        for s in range(2):
+            residual(2, s)
         turn_residual(1)
+        turn_residual(2)
 
         def live(c):
             return 0 <= c < CHUNKS
@@ -486,43 +502,66 @@ def tile_deeparstudentheadgradient_w4_kernel(
         def late(c):
             return live(c) and c != 2
 
-        for i in range(1, CHUNKS + 4):
-            if live(i - 1):
-                inverse_root(i - 1)
+        for i in range(1, CHUNKS):
+            k, blk = (i - 4) % 2, (i - 4) // 2
+            both = (0, 1) if i > 2 else (0,)
+            inverse_root(i - 1)
             if late(i + 1):
                 location(i + 1)
             if i == 1:
                 square_residual(1)
-            if live(i - 3):
-                group_grad(1, i - 3)
-            if live(i - 2):
-                group_grad(0, i - 2)
-            if live(i - 3):
-                quantise_grad(1, i - 3)
             if late(i + 1):
                 residual(i + 1, 0)
+            if live(i - 2):
+                group_grads(i - 2, both)
             if late(i + 1):
                 residual(i + 1, 1)
-            if live(i - 1):
-                scaled_residual(i - 1)
+            scaled_residual(i - 1)
             if live(i - 2):
-                quantise_grad(0, i - 2)
-            k, blk = (i - 4) % 2, (i - 4) // 2
+                quantise_grads(i - 2, both)
             if i >= 4:
                 contract(k, blk)
             if live(i - 2):
                 square_scaled(i - 2)
             if live(i - 2) and (i - 2) in GC_ON_VECTOR:
                 grad_precision(i - 2, True)
-            if live(i - 1):
-                grad_location(i - 1)
+            grad_location(i - 1)
+            if i >= 4:
+                store(k, blk, False, 0)
             if live(i - 2) and (i - 2) not in GC_ON_VECTOR:
                 grad_precision(i - 2, False)
-            if live(i):
-                denominator(i)
+            denominator(i)
             if late(i + 1):
                 turn_residual(i + 1)
             if i >= 4:
-                store(k, blk, i in OUT_ON_VECTOR)
+                store(k, blk, False, 1)
             if live(i + 1):
                 square_residual(i + 1)
+
+        last = CHUNKS - 1
+        blk = last // GROUPS
+        contract(0, blk - 1)
+        inverse_root(last)
+        scaled_residual(last)
+        group_grads(last - 1, (0, 1))
+        square_scaled(last - 1)
+        store(0, blk - 1, False, 0)
+        grad_location(last)
+        quantise_grads(last - 1, (0, 1))
+        contract(1, blk - 1)
+        grad_precision(last - 1, False)
+        square_scaled(last)
+        store(0, blk - 1, False, 1)
+        grad_precision(last, False)
+        group_grads(last, (0,))
+        group_grads(last, (1,))
+        quantise_grads(last, (0,))
+        contract(0, blk)
+        group_grads(last + 1, (1,))
+        quantise_grads(last, (1,))
+        quantise_grads(last + 1, (1,))
+        contract(1, blk)
+        store(1, blk - 1, False)
+        store(0, blk, False)
+        store(1, blk, True, 0)
+        store(1, blk, False, 1)

from contextlib import ExitStack

import concourse.mybir as mybir
from concourse.masks import make_identity

N, D, E, T = 1024, 1024, 512, 1024
FLOPS = 2 * 2 * N * D * T + 2 * 2 * E * N * T

F32 = mybir.dt.float32
BF16 = mybir.dt.bfloat16
I32 = mybir.dt.int32
U32 = mybir.dt.uint32
U8 = mybir.dt.uint8
FP8 = mybir.dt.float8_e4m3fn
FP8X4 = mybir.dt.float8_e4m3fn_x4
FP4X4 = mybir.dt.float4_e2m1fn_x4
ACT = mybir.ActivationFunctionType
ALU = mybir.AluOpType

P = 128
PACK = 4
PASS = P * PACK
GROUPS = N // PASS
K_PASSES = D // PASS
T_TILES = T // P
E_TILES = E // P
WIDTHS = [256, 256, 256, 256]
STARTS = [sum(WIDTHS[:i]) for i in range(len(WIDTHS))]
CHUNKS = len(WIDTHS) * GROUPS
GC_ON_VECTOR = (4,)
OUT_ON_VECTOR = ()
WIDEN_ON_VECTOR = 2
OUT_SCALE = 1.0 / 32.0


def tile_deeparstudentheadgradient_w4_kernel(
    tc, h_bytes, h_scale, e, y, nu, wm_words, wm_scales, ws_words, ws_scales, g, out_0, out_1
):
    nc = tc.nc
    with ExitStack() as ctx:
        keep = ctx.enter_context(tc.tile_pool(name="keep", bufs=1))
        work = ctx.enter_context(tc.tile_pool(name="work", bufs=3))
        psum = ctx.enter_context(tc.psum_pool(name="psum", bufs=1))
        ctx.enter_context(tc.manual_schedule())

        free_banks = list(range(8))
        bank_of = {}

        def bank(*key):
            slot = free_banks[0]
            free_banks.remove(slot)
            bank_of[key] = slot
            return psum.tile([P, PASS], F32, name="%s_bank" % key[0], tag="bank%d" % slot)

        def release(*key):
            free_banks.append(bank_of[key])

        ws_sc = keep.tile([P, K_PASSES, T], U8, name="ws_sc", align_bytes=64)
        wm_sc = keep.tile([P, K_PASSES, T], U8, name="wm_sc", align_bytes=64)
        nu_rows = keep.tile([P, 2, P], F32, name="nu_rows")
        nc.vector.memset(ws_sc[:].bitcast(I32), 0)
        nc.vector.memset(nu_rows[:], 0.0)
        nc.vector.memset(wm_sc[:].bitcast(I32), 0)
        ident = keep.tile([P, P], F32, name="ident")
        make_identity(nc, ident[:])

        h_rows = h_bytes.rearrange("(g p jj j) k -> g jj p (j k)", g=GROUPS, p=P, jj=2)
        h_raw = []

        def load_h(i):
            h_tile = keep.tile([P, 2 * D], U8, name="h_raw%d" % i)
            nc.sync.dma_start(out=h_tile[:], in_=h_rows[i // 2, i % 2])
            h_raw.append(h_tile)

        def load_scales(queue, scales, plane):
            for q in range(4):
                queue.dma_start(
                    out=plane[32 * q : 32 * q + 4, :, :].bitcast(I32),
                    in_=scales[:, 4 * q : 4 * q + 4, :].rearrange("a r n -> r a n").bitcast(I32),
                )

        def load_words(words, name):
            w_tile = keep.tile([P, K_PASSES, 2 * T], U8, name=name, align_bytes=64)
            nc.sync.dma_start(out=w_tile[:].bitcast(I32), in_=words.rearrange("a p n -> p a n").bitcast(I32))
            return w_tile

        nu_raw = keep.tile([T_TILES, P], BF16, name="nu_raw")
        nc.sync.dma_start(out=nu_raw[:], in_=nu.rearrange("(b p) -> b p", p=P))
        load_h(0)
        hs_k = keep.tile([P, K_PASSES, PACK], F32, name="hs_k")
        nc.sync.dma_start(out=hs_k[:], in_=h_scale.rearrange("o (a p j) -> p (o a) j", a=K_PASSES, j=PACK))
        for i in range(1, 4):
            load_h(i)
        ws_w = load_words(ws_words, "ws_w")
        g_raw = keep.tile([P, GROUPS, PACK], BF16, name="g_raw")
        nc.sync.dma_start(out=g_raw[:], in_=g.rearrange("(g p j) -> p g j", g=GROUPS, j=PACK))
        load_scales(nc.sync, ws_scales, ws_sc)
        load_scales(nc.sync, wm_scales, wm_sc)
        wm_w = load_words(wm_words, "wm_w")

        y_sb = []
        e_sb = []
        y_rows = y.rearrange("(g p j) t -> g p j t", g=GROUPS, j=PACK)
        e_rows = e.rearrange("(g p j) m -> g p j m", g=GROUPS, j=PACK)
        for gi in range(GROUPS):
            y_tile = keep.tile([P, PACK, T], BF16, name="y_sb%d" % gi)
            nc.sync.dma_start(out=y_tile[:], in_=y_rows[gi])
            y_sb.append(y_tile)
            e_tile = keep.tile([P, PACK, E], BF16, name="e_sb%d" % gi)
            nc.sync.dma_start(out=e_tile[:], in_=e_rows[gi])
            e_sb.append(e_tile)

        nu_cols = keep.tile([P, 2, T_TILES], F32, name="nu_cols")
        nu_one = keep.tile([P, T_TILES], F32, name="nu_one")
        nu_inv = keep.tile([P, T_TILES], F32, name="nu_inv")
        nu_ratio = keep.tile([P, T_TILES], F32, name="nu_ratio")
        nu_log = keep.tile([P, T_TILES], F32, name="nu_log")
        root0 = keep.tile([P, T_TILES], F32, name="root0")
        root_t = keep.tile([P, T_TILES], F32, name="root_t")
        root = keep.tile([P, T_TILES], F32, name="root")
        nc.scalar.activation(out=nu_rows[0:T_TILES, 1, :], in_=nu_raw[:], func=ACT.Ln, bias=1.0)
        nc.vector.tensor_copy(out=nu_rows[0:T_TILES, 0, :], in_=nu_raw[:])
        nu_bank = bank("nu")
        for s in range(2):
            nc.tensor.transpose(nu_bank[:, P * s : P * (s + 1)], nu_rows[:, s, :], ident[:])

        def nu_step(s):
            if s == 0:
                turned = nu_bank[:, 0 : 2 * P].rearrange("p (s b) -> p s b", s=2)
                nc.vector.tensor_copy(out=nu_cols[:], in_=turned[:, :, 0:T_TILES])
                nc.vector.tensor_scalar(
                    out=nu_one[:], in0=nu_bank[:, 0:T_TILES], scalar1=1.0, scalar2=None, op0=ALU.add
                )
                release("nu")
            if s == 1:
                nc.vector.reciprocal(out=nu_inv[:], in_=nu_one[:])
            if s == 2:
                nc.vector.tensor_tensor(out=nu_ratio[:], in0=nu_cols[:, 0, :], in1=nu_inv[:], op=ALU.mult)

        def log_ratio():
            nc.scalar.activation(out=nu_log[:], in_=nu_ratio[:], func=ACT.Ln)

        def guess_root():
            nc.scalar.activation(out=root0[:], in_=nu_cols[:, 1, :], func=ACT.Exp, scale=-0.5)

        def polish_root(s):
            if s == 0:
                nc.vector.tensor_tensor(out=root_t[:], in0=root0[:], in1=root0[:], op=ALU.mult)
            if s == 1:
                nc.vector.scalar_tensor_tensor(
                    out=root_t[:], in0=root_t[:], scalar=-0.5, in1=nu_one[:], op0=ALU.mult, op1=ALU.mult
                )
            if s == 2:
                nc.vector.scalar_tensor_tensor(
                    out=root[:], in0=root_t[:], scalar=1.5, in1=root0[:], op0=ALU.add, op1=ALU.mult
                )

        g_pos = keep.tile([P, GROUPS, PACK], F32, name="g_pos")
        g_neg = keep.tile([P, GROUPS, PACK], F32, name="g_neg")

        def widen_g():
            nc.vector.tensor_copy(out=g_pos[:], in_=g_raw[:])
            nc.vector.tensor_scalar(out=g_neg[:], in0=g_raw[:], scalar1=-1.0, scalar2=None, op0=ALU.mult)

        h_codes = [keep.tile([P, K_PASSES, PASS], U32, name="h_codes%d" % gi, align_bytes=64) for gi in range(GROUPS)]
        h_planes = [keep.tile([P, K_PASSES, PASS], U8, name="h_planes%d" % gi, align_bytes=64) for gi in range(GROUPS)]
        h_wide = {}
        h_turned = {}
        h_banks = {}

        def widen_h(i):
            wide = work.tile([P, D], BF16, name="h_wide", tag="h_wide", bufs=4)
            j = i % 2
            codes = h_raw[i // 2][:, D * j : D * (j + 1)].bitcast(FP8)
            if i < WIDEN_ON_VECTOR:
                nc.vector.tensor_copy(out=wide[:], in_=codes)
            else:
                nc.scalar.copy(out=wide[:], in_=codes)
            h_wide[i] = wide

        def turn_h(i):
            words = h_wide[i][:].bitcast(F32)
            turned = bank("h", i)
            for a in range(K_PASSES):
                for u in range(2):
                    s = K_PASSES * u + a
                    nc.tensor.transpose(
                        turned[:, P * s : P * (s + 1)], words[:, 256 * a + u : 256 * (a + 1) : 2], ident[:]
                    )
            h_banks[i] = turned

        def scale_h(i):
            if i % 2 == 0:
                h_turned[i // 2] = work.tile(
                    [P, K_PASSES, 2, P * PACK], BF16, name="h_grouped", tag="h_grouped", bufs=2, align_bytes=64
                )
            nc.vector.tensor_tensor(
                out=h_turned[i // 2][:, :, i % 2, :].rearrange("p a (r u v) -> p a r u v", u=2, v=2),
                in0=h_banks[i][:].bitcast(BF16).rearrange("p (u a r v) -> p a r u v", u=2, a=K_PASSES, v=2),
                in1=hs_k[:].rearrange("p a (u v) -> p a u v", u=2).unsqueeze(2).to_broadcast([P, K_PASSES, P, 2, 2]),
                op=ALU.mult,
            )
            release("h", i)

        def quantise_h(pair, a):
            gi, jj = divmod(pair, 2)
            cols = slice(2 * P * jj, 2 * P * (jj + 1))
            nc.vector.quantize_mx(
                out=h_codes[gi][:, a, cols].bitcast(FP8X4),
                scales=h_planes[gi][:, a, cols],
                in_=h_turned[pair][:, a, :, :].rearrange("p j x -> p (j x)"),
            )

        nq = {}

        def log_precision(b, gi):
            acc = bank("c", b, gi)
            for a in range(K_PASSES):
                nc.tensor.matmul_mx(
                    out=acc[:],
                    lhsT=ws_w[:, a, 2 * P * b : 2 * P * (b + 1)].bitcast(FP4X4),
                    lhsT_scale=ws_sc[:, a, P * b : P * (b + 1)],
                    rhs=h_codes[gi][:, a, :].bitcast(FP8X4),
                    rhs_scale=h_planes[gi][:, a, :],
                    start=(a == 0),
                    stop=(a == K_PASSES - 1),
                )
            term = keep.tile([P, PASS], F32, name="nq%d_%d" % (b, gi))
            nc.scalar.activation(out=term[:], in_=acc[:], func=ACT.Exp, scale=-2.0, bias=nu_log[:, b : b + 1])
            release("c", b, gi)
            nq[b, gi] = term

        e_codes = [keep.tile([P, E], U32, name="e_codes%d" % gi, align_bytes=64) for gi in range(GROUPS)]
        e_planes = [keep.tile([P, E], U8, name="e_planes%d" % gi, align_bytes=64) for gi in range(GROUPS)]
        e_grouped = [keep.tile([P, E, PACK], BF16, name="e_grouped%d" % gi, align_bytes=64) for gi in range(GROUPS)]

        def interleave(dst, src):
            nc.vector.tensor_copy(
                out=dst[:].rearrange("p (c i) j -> p c j i", i=4), in_=src[:].rearrange("p j (c i) -> p c j i", i=4)
            )

        def quantise(codes, plane, grouped):
            nc.vector.quantize_mx(
                out=codes[:].bitcast(FP8X4), scales=plane[:], in_=grouped[:].rearrange("p c j -> p (c j)")
            )

        a_banks = {}
        d_sb = {}
        d2_sb = {}
        dt_banks = {}
        den_banks = {}
        rs_sb = {}
        u_sb = {}
        u2_sb = {}
        grads = {}
        grouped_grads = {}
        quantised = {}
        out_banks = {}

        def tiles_of(c):
            blk = c // GROUPS
            return range(STARTS[blk] // P, (STARTS[blk] + WIDTHS[blk]) // P)

        def width(c):
            return WIDTHS[c // GROUPS]

        def location(c, rows=range(PACK)):
            gi = c % GROUPS
            if 0 in rows:
                a_banks[c] = [bank("a", b, gi) for b in tiles_of(c)]
            for acc, b in zip(a_banks[c], tiles_of(c)):
                for j in rows:
                    for a in range(K_PASSES):
                        nc.tensor.matmul_mx(
                            out=acc[:, P * j : P * (j + 1)],
                            lhsT=h_codes[gi][:, a, P * j : P * (j + 1)].bitcast(FP8X4),
                            lhsT_scale=h_planes[gi][:, a, P * j : P * (j + 1)],
                            rhs=wm_w[:, a, 2 * P * b : 2 * P * (b + 1)].bitcast(FP4X4),
                            rhs_scale=wm_sc[:, a, P * b : P * (b + 1)],
                            start=(a == 0),
                            stop=(a == K_PASSES - 1),
                        )

        def residual(c, s):
            gi = c % GROUPS
            if s >= len(tiles_of(c)):
                return
            if s == 0:
                d_sb[c] = work.tile([P, PACK, width(c)], F32, name="d_sb", tag="d_sb", bufs=4)
            b = tiles_of(c)[s]
            nc.vector.tensor_tensor(
                out=d_sb[c][:, :, P * s : P * (s + 1)],
                in0=a_banks[c][s][:].rearrange("p (j t) -> p j t", j=PACK),
                in1=y_sb[gi][:, :, P * b : P * (b + 1)],
                op=ALU.subtract,
            )
            release("a", b, gi)

        def turn_residual(c):
            dt_banks[c] = []
            for s in range(len(tiles_of(c))):
                turned = bank("dt", c, s)
                for j in range(PACK):
                    nc.tensor.transpose(turned[:, P * j : P * (j + 1)], d_sb[c][:, j, P * s : P * (s + 1)], ident[:])
                dt_banks[c].append(turned)

        def square_residual(c):
            d2_sb[c] = []
            for s, b in enumerate(tiles_of(c)):
                sq = work.tile([P, PASS], F32, name="d2_sb", tag="d2_sb", bufs=4)
                nc.scalar.activation(out=sq[:], in_=dt_banks[c][s][:], func=ACT.Square, scale=root[:, b : b + 1])
                release("dt", c, s)
                d2_sb[c].append(sq)

        def denominator(c):
            gi = c % GROUPS
            den_banks[c] = []
            for s, b in enumerate(tiles_of(c)):
                acc = bank("den", c, s)
                for j in range(PACK):
                    cols = slice(P * j, P * (j + 1))
                    nc.tensor.matmul(
                        acc[:, cols], lhsT=nq[b, gi][:, cols], rhs=ident[:], start=True, stop=False, is_transpose=True
                    )
                    nc.tensor.matmul(
                        acc[:, cols], lhsT=d2_sb[c][s][:, cols], rhs=ident[:], start=False, stop=True, is_transpose=True
                    )
                den_banks[c].append(acc)

        def inverse_root(c):
            rs_sb[c] = work.tile([P, PACK, width(c)], F32, name="rs_sb", tag="rs_sb")
            for s in range(len(tiles_of(c))):
                nc.scalar.activation(
                    out=rs_sb[c][:, :, P * s : P * (s + 1)],
                    in_=den_banks[c][s][:].rearrange("p (j t) -> p j t", j=PACK),
                    func=ACT.Abs_reciprocal_sqrt,
                )
                release("den", c, s)

        def scaled_residual(c):
            u_sb[c] = work.tile([P, PACK, width(c)], F32, name="u_sb", tag="u_sb")
            nc.vector.tensor_tensor(out=u_sb[c][:], in0=d_sb[c][:], in1=rs_sb[c][:], op=ALU.mult)

        def open_pair(s):
            if s not in grads:
                grads[s] = work.tile([P, 2, PACK, WIDTHS[0]], BF16, name="grads", tag="grads")

        def grad_location(c):
            gi = c % GROUPS
            open_pair(c)
            for j in range(PACK):
                nc.vector.scalar_tensor_tensor(
                    out=grads[c][:, 0, j, :],
                    in0=u_sb[c][:, j, :],
                    scalar=g_pos[:, gi, j : j + 1],
                    in1=rs_sb[c][:, j, :],
                    op0=ALU.mult,
                    op1=ALU.mult,
                )

        def square_scaled(c):
            u2 = work.tile([P, PACK, width(c)], F32, name="u2", tag="u2")
            nc.scalar.activation(out=u2[:], in_=u_sb[c][:], func=ACT.Square)
            u2_sb[c] = u2

        def grad_precision(c, on_vector):
            gi = c % GROUPS
            open_pair(c + 1)
            for j in range(PACK):
                if on_vector:
                    nc.vector.tensor_scalar(
                        out=grads[c + 1][:, 1, j, :],
                        in0=u2_sb[c][:, j, :],
                        scalar1=g_pos[:, gi, j : j + 1],
                        scalar2=g_neg[:, gi, j : j + 1],
                        op0=ALU.mult,
                        op1=ALU.add,
                    )
                else:
                    nc.scalar.activation(
                        out=grads[c + 1][:, 1, j, :],
                        in_=u2_sb[c][:, j, :],
                        func=ACT.Identity,
                        scale=g_pos[:, gi, j : j + 1],
                        bias=g_neg[:, gi, j : j + 1],
                    )

        def group_grads(c, ks):
            grouped = work.tile(
                [P, len(ks), WIDTHS[0], PACK], BF16, name="g_grouped", tag="g_grouped", bufs=3, align_bytes=64
            )
            nc.vector.tensor_copy(
                out=grouped[:].rearrange("p k (c i) j -> p k c j i", i=4),
                in_=grads[c][:, ks[0] : ks[-1] + 1, :, :].rearrange("p k j (c i) -> p k c j i", i=4),
            )
            grouped_grads[c, ks] = grouped

        def quantise_grads(c, ks):
            codes = work.tile([P, len(ks), WIDTHS[0]], U32, name="g_codes", tag="g_codes", bufs=5, align_bytes=64)
            plane = work.tile([P, len(ks), WIDTHS[0]], U8, name="g_plane", tag="g_plane", bufs=5, align_bytes=64)
            nc.vector.quantize_mx(
                out=codes[:].rearrange("p k t -> p (k t)").bitcast(FP8X4),
                scales=plane[:].rearrange("p k t -> p (k t)"),
                in_=grouped_grads[c, ks][:].rearrange("p k t j -> p (k t j)"),
            )
            for s, k in enumerate(ks):
                quantised[k, c - k] = (codes[:, s, :], plane[:, s, :])

        def contract(k, blk):
            w = WIDTHS[blk]
            per_bank = PASS // w
            out_banks[k, blk] = []
            for mp in range(E_TILES // per_bank):
                acc = bank("out", k, blk, mp)
                for mm in range(per_bank):
                    m = per_bank * mp + mm
                    for gi in range(GROUPS):
                        codes, plane = quantised[k, blk * GROUPS + gi]
                        nc.tensor.matmul_mx(
                            out=acc[:, w * mm : w * (mm + 1)],
                            lhsT=e_codes[gi][:, P * m : P * (m + 1)].bitcast(FP8X4),
                            lhsT_scale=e_planes[gi][:, P * m : P * (m + 1)],
                            rhs=codes.bitcast(FP8X4),
                            rhs_scale=plane,
                            start=(gi == 0),
                            stop=(gi == GROUPS - 1),
                        )
                out_banks[k, blk].append(acc)

        def store(k, blk, on_vector, only=None):
            w = WIDTHS[blk]
            per_bank = PASS // w
            dst = (out_0, out_1)[k].rearrange("(mp mm p) t -> mp p mm t", mm=per_bank, p=P)
            for mp in range(E_TILES // per_bank):
                if only is not None and mp % 2 != only:
                    continue
                result = work.tile([P, per_bank, w], F32, name="result", tag="result", bufs=6)
                sums = out_banks[k, blk][mp][:].rearrange("p (mm t) -> p mm t", mm=per_bank)
                if on_vector:
                    nc.vector.tensor_scalar(out=result[:], in0=sums, scalar1=OUT_SCALE, scalar2=None, op0=ALU.mult)
                else:
                    nc.scalar.activation(out=result[:], in_=sums, func=ACT.Copy, scale=OUT_SCALE)
                release("out", k, blk, mp)
                nc.sync.dma_start(out=dst[mp, :, :, STARTS[blk] : STARTS[blk] + w], in_=result[:])

        tiles = GROUPS * PACK
        widen_h(0)
        turn_h(0)
        nu_step(0)
        widen_h(1)
        nu_step(1)
        turn_h(1)
        widen_h(2)
        for i in range(tiles):
            if i + 3 < tiles:
                widen_h(i + 3)
            if i + 2 < tiles and i < PACK:
                turn_h(i + 2)
            if i == PACK:
                turn_h(6)
                turn_h(7)
                guess_root()
                for b in range(T_TILES):
                    log_precision(b, 0)
                location(0)
            scale_h(i)
            if i == 0:
                nu_step(2)
                log_ratio()
            if i > PACK:
                polish_root(i - PACK - 1)
            if i == tiles - 1:
                widen_g()
            if i % PACK >= 2:
                for a in range(K_PASSES):
                    quantise_h(i // 2 - 1 + i % 2, a)
        for s in range(2):
            residual(0, s)
        for b in range(3):
            log_precision(b, 1)
        turn_residual(0)
        square_residual(0)
        for gi in range(GROUPS):
            interleave(e_grouped[gi], e_sb[gi])
        for gi in range(GROUPS):
            quantise(e_codes[gi], e_planes[gi], e_grouped[gi])
        for b in range(3, T_TILES):
            log_precision(b, 1)
        location(1)
        for s in range(2):
            residual(1, s)
        denominator(0)
        location(2)
        for s in range(2):
            residual(2, s)
        turn_residual(1)
        turn_residual(2)

        def live(c):
            return 0 <= c < CHUNKS

        def late(c):
            return live(c) and c != 2

        for i in range(1, CHUNKS):
            k, blk = (i - 4) % 2, (i - 4) // 2
            both = (0, 1) if i > 2 else (0,)
            inverse_root(i - 1)
            if late(i + 1):
                location(i + 1)
            if i == 1:
                square_residual(1)
            if late(i + 1):
                residual(i + 1, 0)
            if live(i - 2):
                group_grads(i - 2, both)
            if late(i + 1):
                residual(i + 1, 1)
            scaled_residual(i - 1)
            if live(i - 2):
                quantise_grads(i - 2, both)
            if i >= 4:
                contract(k, blk)
            if live(i - 2):
                square_scaled(i - 2)
            if live(i - 2) and (i - 2) in GC_ON_VECTOR:
                grad_precision(i - 2, True)
            grad_location(i - 1)
            if i >= 4:
                store(k, blk, False, 0)
            if live(i - 2) and (i - 2) not in GC_ON_VECTOR:
                grad_precision(i - 2, False)
            denominator(i)
            if late(i + 1):
                turn_residual(i + 1)
            if i >= 4:
                store(k, blk, False, 1)
            if live(i + 1):
                square_residual(i + 1)

        last = CHUNKS - 1
        blk = last // GROUPS
        contract(0, blk - 1)
        inverse_root(last)
        scaled_residual(last)
        group_grads(last - 1, (0, 1))
        square_scaled(last - 1)
        store(0, blk - 1, False, 0)
        grad_location(last)
        quantise_grads(last - 1, (0, 1))
        contract(1, blk - 1)
        grad_precision(last - 1, False)
        square_scaled(last)
        store(0, blk - 1, False, 1)
        grad_precision(last, False)
        group_grads(last, (0,))
        group_grads(last, (1,))
        quantise_grads(last, (0,))
        contract(0, blk)
        group_grads(last + 1, (1,))
        quantise_grads(last, (1,))
        quantise_grads(last + 1, (1,))
        contract(1, blk)
        store(1, blk - 1, False)
        store(0, blk, False)
        store(1, blk, True, 0)
        store(1, blk, False, 1)
